import numpy as np
import ml_dtypes


def mxq(x, axis, fmt="e4m3"):
    dtype, down = {"e4m3": (ml_dtypes.float8_e4m3fn, 7), "e5m2": (ml_dtypes.float8_e5m2, 14)}[fmt]
    v = np.moveaxis(np.asarray(x, np.float32).astype(ml_dtypes.bfloat16).astype(np.float64), axis, -1)
    blocks = v.reshape(v.shape[:-1] + (-1, 32))
    amax = np.abs(blocks).max(-1, keepdims=True)
    byte = np.maximum(np.where(amax > 0, np.frexp(amax)[1] - 1 + 127, 0) - down, 1)
    scale = np.exp2(byte - 127.0)
    codes = (blocks / scale).astype(np.float32).astype(dtype).astype(np.float64)
    return np.moveaxis((codes * scale).reshape(v.shape), -1, axis)


WIDE = False


def mx_kscale(k):
    if not WIDE:
        return np.ones(k)
    levels = np.array([10, -10, 5, -5, 0])
    if k % 512:
        return np.exp2(np.random.permutation(np.resize(levels, k // 32))).repeat(32)
    a = np.empty((k // 512, 16))
    for p in range(k // 512):
        a[p, :8] = np.random.permutation(np.resize(levels, 8))
        for g in range(8):
            far = levels[np.abs(levels - a[p, g]) >= 10]
            a[p, g + 8] = far[np.random.randint(len(far))]
    return np.exp2(a.ravel()).repeat(32)


BF16 = ml_dtypes.bfloat16


def bf(x):
    return np.asarray(x, np.float32).astype(BF16)


def f64(x):
    return np.asarray(x).astype(np.float64)


E2M1 = np.array([0.0, 0.5, 1.0, 1.5, 2.0, 3.0, 4.0, 6.0, -0.0, -0.5, -1.0, -1.5, -2.0, -3.0, -4.0, -6.0])


def pack_weight(w, fmt):
    k, n = w.shape
    w = f64(bf(w)).reshape(k // 32, 32, n)
    amax = np.abs(w).max(1)
    if fmt == "e4m3":
        byte = np.frexp(amax)[1] - 1 + 127 - 7
    else:
        mant, ex = np.frexp(amax / 6.0)
        byte = np.where(mant > 0.5, ex, ex - 1) + 127
    byte = np.clip(np.where(amax > 0, byte, 1), 1, 254)
    scaled = (w * np.exp2(127.0 - byte)[:, None, :]).reshape(k, n).astype(np.float32)
    by_word = np.ascontiguousarray(scaled.reshape(k // 512, 128, 4, n).transpose(0, 1, 3, 2))
    if fmt == "e4m3":
        words = by_word.astype(ml_dtypes.float8_e4m3fn).view(np.uint8)
    else:
        c = by_word.astype(ml_dtypes.float4_e2m1fn).view(np.uint8) & 0xF
        words = c[..., 0::2] | (c[..., 1::2] << 4)
    return np.ascontiguousarray(words), np.ascontiguousarray(byte.astype(np.uint8).reshape(k // 512, 16, n))


def unpack_weight(words, scales, fmt):
    g, p, n, _ = words.shape
    if fmt == "e4m3":
        vals = np.ascontiguousarray(words).view(ml_dtypes.float8_e4m3fn).astype(np.float64)
    else:
        nib = np.empty((g, p, n, 4), np.uint8)
        nib[..., 0::2] = words & 0xF
        nib[..., 1::2] = words >> 4
        vals = E2M1[nib]
    vals = vals * np.repeat(np.exp2(scales.astype(np.float64) - 127.0), 8, axis=1)[..., None]
    return vals.transpose(0, 1, 3, 2).reshape(g * 512, n)
def pack4(w):
    words, scales = pack_weight(w, "e2m1")
    return words.reshape(words.shape[0], 128, -1), scales


def unpack4(words, scales):
    return unpack_weight(words.reshape(words.shape[0], 128, -1, 2), scales, "e2m1")


G, H, W = 4, 1024, 512


def setup_inputs():
    s = mx_kscale(G * H).reshape(G, H)
    t = mx_kscale(G * W).reshape(G, W)
    i, j = np.arange(H), np.arange(W)
    near_i = np.exp(-2.0 * np.abs(i[:, None] - i) / H)
    near_j = np.exp(-2.0 * np.abs(j[:, None] - j) / W)
    grid = np.random.standard_normal((G, H, W)) * s[:, :, None] * t[:, None, :]
    ceiling = (0.7 + 0.1 * np.random.standard_normal((G, W))) * t
    rk = 1.6 * np.random.standard_normal((G, H, H)) * near_i / np.sqrt(H) / s[:, :, None]
    ck = 1.6 * np.random.standard_normal((G, W, W)) * near_j / np.sqrt(W) / t[:, :, None]
    row_words, row_scales = pack4(rk.reshape(G * H, H))
    col_words, col_scales = pack4(ck.reshape(G * W, W))
    return {"grid": bf(grid),
            "row_words": row_words, "row_scales": row_scales,
            "ceiling": bf(ceiling),
            "col_words": col_words, "col_scales": col_scales,
            "base": bf(0.3 * np.random.standard_normal((G, W)))}


def reference(grid, row_words, row_scales, ceiling, col_words, col_scales, base):
    rk = unpack4(row_words, row_scales).reshape(G, H, H)
    ck = unpack4(col_words, col_scales).reshape(G, W, W)
    spread = rk.transpose(0, 2, 1) @ mxq(f64(grid), 1, "e4m3")
    capped = np.minimum(spread, f64(ceiling)[:, None, :])
    cost = mxq(capped, 2, "e4m3") @ ck
    return np.tanh(cost + f64(base)[:, None, :])

@@ -1,0 +1,249 @@
+from contextlib import ExitStack
+
+import concourse.mybir as mybir
+
+LAYERS, ROWS, COLS = 4, 1024, 512
+FLOPS = 2 * LAYERS * (ROWS * ROWS * COLS + ROWS * COLS * COLS)
+
+F32 = mybir.dt.float32
+BF16 = mybir.dt.bfloat16
+I32 = mybir.dt.int32
+U32 = mybir.dt.uint32
+U8 = mybir.dt.uint8
+E4M3 = mybir.dt.float8_e4m3fn_x4
+E2M1 = mybir.dt.float4_e2m1fn_x4
+MIN = mybir.AluOpType.min
+ADD = mybir.AluOpType.add
+TANH = mybir.ActivationFunctionType.Tanh
+
+P = 128
+X4 = 4
+GROUPS = ROWS // 512
+PAIRS = 16
+PER_LAYER = 4
+
+S_PIECES_FIRST = (1, 3, 5, 7)
+S_PIECES = (2, 5, 7)
+LEAD, SPAN = 3.9, 2.3
+V_DIRECT = ((0, 0), (0, 1), (13, 0), (14, 1))
+
+
+def tile_layered_costmap_spreading_s14_kernel(
+    tc, grid, row_words, row_scales, ceiling, col_words, col_scales, base, out
+):
+    nc = tc.nc
+    steps = []
+
+    def at(key, fn, *args):
+        steps.append((key, len(steps), fn, args))
+
+    with ExitStack() as ctx:
+        keep = ctx.enter_context(tc.tile_pool(name="keep", bufs=1))
+        ring = ctx.enter_context(tc.tile_pool(name="ring", bufs=4))
+        psum = ctx.enter_context(tc.psum_pool(name="psum", bufs=4))
+
+        raw = [keep.tile([P, GROUPS, X4, COLS], BF16, name="raw%d" % l, align_bytes=64) for l in range(LAYERS)]
+        rw = [keep.tile([P, GROUPS, 2 * ROWS], U8, name="rw%d" % l, align_bytes=64) for l in range(LAYERS)]
+        rs0 = keep.tile([P, GROUPS, ROWS], U8, name="rs0", align_bytes=64)
+        rs_rest = keep.tile([P, (LAYERS - 1) * GROUPS, ROWS], U8, name="rs_rest", align_bytes=64)
+        cw0 = keep.tile([P, 2 * COLS], U8, name="cw0", align_bytes=64)
+        cw_rest = keep.tile([P, LAYERS - 1, 2 * COLS], U8, name="cw_rest", align_bytes=64)
+        cs = keep.tile([P, LAYERS, COLS], U8, name="cs", align_bytes=64)
+        ceil_sb = keep.tile([P, LAYERS, X4], BF16, name="ceil_sb", align_bytes=64)
+        base_sb = [keep.tile([P, COLS], BF16, name="base%d" % l, align_bytes=64) for l in range(LAYERS)]
+        gcodes = [keep.tile([P, GROUPS, COLS], U32, name="gcodes%d" % l, align_bytes=64) for l in range(LAYERS)]
+        gscales = [keep.tile([P, GROUPS, COLS], U8, name="gscales%d" % l, align_bytes=64) for l in range(LAYERS)]
+        warm = keep.tile([P, 1], F32, name="warm")
+
+        gin = {}
+        ps1 = {}
+        ps2 = {}
+        spread = {}
+        capped = {}
+        ccodes = {}
+        cscales = {}
+        sums = {}
+
+        def scale_rows(plane, source, r):
+            nc_rows = source.rearrange("g (q r) n -> r q g n", r=4)[r]
+            return plane[r:P:32], nc_rows
+
+        def setup():
+            nc.vector.memset(rs0[:].rearrange("p g n -> p (g n)").bitcast(U32), 0)
+            nc.vector.memset(warm[:], 0.0)
+            nc.gpsimd.memset(cs[:].rearrange("p g n -> p (g n)").bitcast(U32), 0)
+            nc.gpsimd.memset(rs_rest[:].rearrange("p g n -> p (g n)").bitcast(U32), 0)
+            nc.scalar.activation(warm[:], warm[:], TANH)
+
+        def load_scales(engine, plane, source):
+            for r in range(4):
+                o, i = scale_rows(plane, source, r)
+                engine.dma_start(out=o.bitcast(I32), in_=i.bitcast(I32))
+
+        def load_grid(l, g):
+            nc.sync.dma_start(
+                out=raw[l][:, g], in_=grid[l, 512 * g : 512 * (g + 1), :].rearrange("(p j) c -> p j c", j=X4)
+            )
+
+        def load_rows(l):
+            nc.sync.dma_start(
+                out=rw[l][:], in_=row_words[GROUPS * l : GROUPS * (l + 1)].rearrange("g p n -> p g n")
+            )
+
+        def load_base(l):
+            nc.sync.dma_start(out=base_sb[l][:], in_=base[l].partition_broadcast(P))
+
+        def loads():
+            load_grid(0, 0)
+            load_grid(0, 1)
+            load_scales(nc.scalar, rs0, row_scales[0:GROUPS])
+            load_rows(0)
+            nc.sync.dma_start(out=ceil_sb[:], in_=ceiling.rearrange("l (p t) -> p l t", t=X4))
+            nc.sync.dma_start(out=cw0[:], in_=col_words[0])
+            load_scales(nc.sync, cs, col_scales)
+            load_base(0)
+            load_grid(1, 0)
+            load_grid(1, 1)
+            load_rows(1)
+            load_scales(nc.sync, rs_rest, row_scales[GROUPS:])
+            nc.sync.dma_start(out=cw_rest[:], in_=col_words[1:].rearrange("l p n -> p l n"))
+            load_base(1)
+            for l in (2, 3):
+                load_grid(l, 0)
+                load_grid(l, 1)
+                load_rows(l)
+                load_base(l)
+
+        def interleave(l, g, t):
+            if t == 0:
+                gin[l, g] = ring.tile([P, X4, P, X4], BF16, name="gin", align_bytes=64)
+            dst = gin[l, g][:, t]
+            src = raw[l][:, g].rearrange("p j (m t) -> p t m j", t=X4)[:, t]
+            if 4 * g + t in (S_PIECES if l else S_PIECES_FIRST):
+                nc.scalar.copy(out=dst, in_=src)
+            else:
+                nc.vector.tensor_copy(out=dst, in_=src)
+
+        def quantize_grid(l, g, h):
+            cols = slice(256 * h, 256 * (h + 1))
+            nc.vector.quantize_mx(
+                out=gcodes[l][:, g, cols].bitcast(E4M3),
+                scales=gscales[l][:, g, cols],
+                in_=gin[l, g][:, 2 * h : 2 * h + 2].rearrange("p t m j -> p (t m j)"),
+            )
+
+        def stage1(k, b):
+            l = k // PER_LAYER
+            n0 = 256 * (k % PER_LAYER) + P * b
+            acc = psum.tile([P, X4, P], F32, name="acc1")
+            ps1[k, b] = acc
+            for t in range(X4):
+                for g in range(GROUPS):
+                    plane = rs0[:, g, n0 : n0 + P] if l == 0 else rs_rest[:, GROUPS * (l - 1) + g, n0 : n0 + P]
+                    nc.tensor.matmul_mx(
+                        out=acc[:, t, :],
+                        lhsT=gcodes[l][:, g, P * t : P * (t + 1)].bitcast(E4M3),
+                        lhsT_scale=gscales[l][:, g, P * t : P * (t + 1)],
+                        rhs=rw[l][:, g, 2 * n0 : 2 * (n0 + P)].bitcast(E2M1),
+                        rhs_scale=plane,
+                        start=(g == 0),
+                        stop=(g == GROUPS - 1),
+                    )
+
+        def leave(k, b):
+            l = k // PER_LAYER
+            if b == 0:
+                capped[k] = ring.tile([P, 2, P, X4], BF16, name="capped", align_bytes=64)
+                spread[k] = ring.tile([P, 2, P, X4], BF16, name="spread", align_bytes=64)
+            src = ps1[k, b][:].rearrange("p t n -> p n t")
+            if (k, b) in V_DIRECT:
+                nc.vector.tensor_tensor(
+                    out=capped[k][:, b], in0=src, in1=ceil_sb[:, l, :].unsqueeze(1).to_broadcast([P, P, X4]), op=MIN
+                )
+            else:
+                nc.scalar.copy(out=spread[k][:, b], in_=src)
+
+        def cap(k):
+            l = k // PER_LAYER
+            bs = [b for b in (0, 1) if (k, b) not in V_DIRECT]
+            if bs:
+                lo, hi = bs[0], bs[-1] + 1
+                n = P * (hi - lo)
+                nc.vector.tensor_tensor(
+                    out=capped[k][:, lo:hi].rearrange("p b n t -> p (b n) t"),
+                    in0=spread[k][:, lo:hi].rearrange("p b n t -> p (b n) t"),
+                    in1=ceil_sb[:, l, :].unsqueeze(1).to_broadcast([P, n, X4]),
+                    op=MIN,
+                )
+
+        def quantize_capped(k):
+            ccodes[k] = ring.tile([P, 2 * P], U32, name="ccodes", align_bytes=64)
+            cscales[k] = ring.tile([P, 2 * P], U8, name="cscales", align_bytes=64)
+            nc.vector.quantize_mx(
+                out=ccodes[k][:].bitcast(E4M3),
+                scales=cscales[k][:],
+                in_=capped[k][:].rearrange("p b n t -> p (b n t)"),
+            )
+
+        def stage2(k, b):
+            l = k // PER_LAYER
+            acc = psum.tile([P, COLS], F32, name="acc2")
+            ps2[k, b] = acc
+            words = cw0[:] if l == 0 else cw_rest[:, l - 1, :]
+            nc.tensor.matmul_mx(
+                out=acc[:],
+                lhsT=ccodes[k][:, P * b : P * (b + 1)].bitcast(E4M3),
+                lhsT_scale=cscales[k][:, P * b : P * (b + 1)],
+                rhs=words.bitcast(E2M1),
+                rhs_scale=cs[:, l, :],
+                start=True,
+                stop=True,
+            )
+
+        def add_base(k, b, c0=0, c1=COLS):
+            l = k // PER_LAYER
+            if b == 0 and c0 == 0:
+                sums[k] = ring.tile([P, 2, COLS], F32, name="sums")
+            nc.vector.tensor_tensor(
+                out=sums[k][:, b, c0:c1], in0=ps2[k, b][:, c0:c1], in1=base_sb[l][:, c0:c1], op=ADD
+            )
+
+        def finish(k, b0=0, b1=2, c0=0, c1=COLS):
+            l = k // PER_LAYER
+            r0 = 256 * (k % PER_LAYER)
+            res = ring.tile([P, 2, COLS], F32, name="res")
+            nc.scalar.activation(res[:, b0:b1, c0:c1], sums[k][:, b0:b1, c0:c1], TANH)
+            nc.sync.dma_start(
+                out=out[l, r0 + P * b0 : r0 + P * b1, c0:c1].rearrange("(b p) c -> p b c", p=P),
+                in_=res[:, b0:b1, c0:c1],
+            )
+
+        at(-9, setup)
+        at(-8, loads)
+        for l in range(LAYERS):
+            for i in range(8):
+                g, t = divmod(i, 4)
+                start, step = (PER_LAYER * l - LEAD, SPAN / 8) if l else (-4, 0.1)
+                at(start + i * step, interleave, l, g, t)
+                if t % 2:
+                    at(start + (i + (2 if l else 1)) * step + 0.001, quantize_grid, l, g, t // 2)
+        for k in range(PAIRS):
+            last = k == PAIRS - 1
+            for b in (0, 1):
+                at(k - 0.95 + 0.01 * b, stage1, k, b)
+                at(k + 0.02 + 0.1 * b, leave, k, b)
+                at(k + 1 + 0.01 * b, stage2, k, b)
+            at(k + 0.6, cap, k)
+            at(k + 0.8, quantize_capped, k)
+            if not last:
+                at(k + 1.4, add_base, k, 0)
+                at(k + 1.9, add_base, k, 1)
+                at(k + 2.3, finish, k)
+            else:
+                for i, (b, c0, c1) in enumerate(((0, 0, 512), (1, 0, 256), (1, 256, 512))):
+                    at(k + 2.4 + 0.1 * i, add_base, k, b, c0, c1)
+                    at(k + 2.45 + 0.1 * i, finish, k, b, b + 1, c0, c1)
+
+        with tc.manual_schedule():
+            for key, order, fn, args in sorted(steps, key=lambda s: s[:2]):
+                fn(*args)

@@ -1,6 +1,7 @@
 from contextlib import ExitStack
 
 import concourse.mybir as mybir
+from concourse.masks import make_identity
 
 LAYERS, ROWS, COLS = 4, 1024, 512
 FLOPS = 2 * LAYERS * (ROWS * ROWS * COLS + ROWS * COLS * COLS)
@@ -22,8 +23,8 @@ GROUPS = ROWS // 512
 PAIRS = 16
 PER_LAYER = 4
 
-S_PIECES_FIRST = (1, 3, 5, 7)
-S_PIECES = (2, 5, 7)
+PIECES_FIRST = ((0, 0, 64), (1, 64, 128))
+PIECES = ((0, 0, 40), (1, 80, 128), (0, 40, 80))
 LEAD, SPAN = 3.9, 2.3
 V_DIRECT = ((0, 0), (0, 1), (13, 0), (14, 1))
 
@@ -50,7 +51,10 @@ def tile_layered_costmap_spreading_s14_kernel(
         cw_rest = keep.tile([P, LAYERS - 1, 2 * COLS], U8, name="cw_rest", align_bytes=64)
         cs = keep.tile([P, LAYERS, COLS], U8, name="cs", align_bytes=64)
         ceil_sb = keep.tile([P, LAYERS, X4], BF16, name="ceil_sb", align_bytes=64)
-        base_sb = [keep.tile([P, COLS], BF16, name="base%d" % l, align_bytes=64) for l in range(LAYERS)]
+        base_sb = keep.tile([P, LAYERS, COLS], BF16, name="base_sb", align_bytes=64)
+        base_col = keep.tile([P, LAYERS, X4], BF16, name="base_col", align_bytes=64)
+        rows = keep.tile([P, COLS], BF16, name="rows", align_bytes=64)
+        ident = keep.tile([P, P], BF16, name="ident", align_bytes=64)
         gcodes = [keep.tile([P, GROUPS, COLS], U32, name="gcodes%d" % l, align_bytes=64) for l in range(LAYERS)]
         gscales = [keep.tile([P, GROUPS, COLS], U8, name="gscales%d" % l, align_bytes=64) for l in range(LAYERS)]
         warm = keep.tile([P, 1], F32, name="warm")
@@ -70,7 +74,9 @@ def tile_layered_costmap_spreading_s14_kernel(
 
         def setup():
             nc.vector.memset(rs0[:].rearrange("p g n -> p (g n)").bitcast(U32), 0)
+            nc.vector.memset(rows[:].bitcast(U32), 0)
             nc.vector.memset(warm[:], 0.0)
+            make_identity(nc, ident[:])
             nc.gpsimd.memset(cs[:].rearrange("p g n -> p (g n)").bitcast(U32), 0)
             nc.gpsimd.memset(rs_rest[:].rearrange("p g n -> p (g n)").bitcast(U32), 0)
             nc.scalar.activation(warm[:], warm[:], TANH)
@@ -90,46 +96,63 @@ def tile_layered_costmap_spreading_s14_kernel(
                 out=rw[l][:], in_=row_words[GROUPS * l : GROUPS * (l + 1)].rearrange("g p n -> p g n")
             )
 
-        def load_base(l):
-            nc.sync.dma_start(out=base_sb[l][:], in_=base[l].partition_broadcast(P))
-
         def loads():
+            nc.sync.dma_start(out=rows[0:LAYERS, :], in_=ceiling)
+            nc.sync.dma_start(out=rows[LAYERS : 2 * LAYERS, :], in_=base)
             load_grid(0, 0)
             load_grid(0, 1)
             load_scales(nc.scalar, rs0, row_scales[0:GROUPS])
             load_rows(0)
-            nc.sync.dma_start(out=ceil_sb[:], in_=ceiling.rearrange("l (p t) -> p l t", t=X4))
-            nc.sync.dma_start(out=cw0[:], in_=col_words[0])
             load_scales(nc.sync, cs, col_scales)
-            load_base(0)
+            nc.sync.dma_start(out=cw0[:], in_=col_words[0])
             load_grid(1, 0)
             load_grid(1, 1)
             load_rows(1)
             load_scales(nc.sync, rs_rest, row_scales[GROUPS:])
             nc.sync.dma_start(out=cw_rest[:], in_=col_words[1:].rearrange("l p n -> p l n"))
-            load_base(1)
             for l in (2, 3):
                 load_grid(l, 0)
                 load_grid(l, 1)
                 load_rows(l)
-                load_base(l)
 
-        def interleave(l, g, t):
-            if t == 0:
+        def turn_vectors():
+            pc = psum.tile([P, X4, P], BF16, name="pc", tag="acc2")
+            pb = psum.tile([P, X4, P], BF16, name="pb", tag="acc2")
+            for t in range(X4):
+                nc.tensor.transpose(pc[:, t, :], rows[:, t:COLS:X4], ident[:])
+            for q in range(X4):
+                nc.tensor.transpose(pb[:, q, :], rows[:, P * q : P * (q + 1)], ident[:])
+            nc.vector.tensor_copy(out=ceil_sb[:], in_=pc[:, :, 0:LAYERS].rearrange("p t l -> p l t"))
+            nc.vector.tensor_copy(out=base_col[:], in_=pb[:, :, LAYERS : 2 * LAYERS].rearrange("p q l -> p l q"))
+
+        spreadb = {}
+
+        def spread_base():
+            for l in range(LAYERS):
+                ps = psum.tile([P, X4, P], BF16, name="ps", tag="acc2")
+                spreadb[l] = ps
+                for q in range(X4):
+                    nc.tensor.transpose(ps[:, q, :], base_col[:, l, q : q + 1].to_broadcast([P, P]), ident[:])
+
+        def keep_base(l):
+            copy = nc.scalar.copy if l % 2 else nc.vector.tensor_copy
+            copy(out=base_sb[:, l, :], in_=spreadb[l][:].rearrange("p q n -> p (q n)"))
+
+        def interleave(l, g, on_scalar, m0, m1):
+            if (l, g) not in gin:
                 gin[l, g] = ring.tile([P, X4, P, X4], BF16, name="gin", align_bytes=64)
-            dst = gin[l, g][:, t]
-            src = raw[l][:, g].rearrange("p j (m t) -> p t m j", t=X4)[:, t]
-            if 4 * g + t in (S_PIECES if l else S_PIECES_FIRST):
+            dst = gin[l, g][:, :, m0:m1, :].rearrange("p t m j -> p m j t")
+            src = raw[l][:, g].rearrange("p j (m t) -> p m j t", t=X4)[:, m0:m1]
+            if on_scalar:
                 nc.scalar.copy(out=dst, in_=src)
             else:
                 nc.vector.tensor_copy(out=dst, in_=src)
 
-        def quantize_grid(l, g, h):
-            cols = slice(256 * h, 256 * (h + 1))
+        def quantize_grid(l, g, c0, c1):
             nc.vector.quantize_mx(
-                out=gcodes[l][:, g, cols].bitcast(E4M3),
-                scales=gscales[l][:, g, cols],
-                in_=gin[l, g][:, 2 * h : 2 * h + 2].rearrange("p t m j -> p (t m j)"),
+                out=gcodes[l][:, g, c0:c1].bitcast(E4M3),
+                scales=gscales[l][:, g, c0:c1],
+                in_=gin[l, g][:].rearrange("p t m j -> p (t m j)")[:, X4 * c0 : X4 * c1],
             )
 
         def stage1(k, b):
@@ -205,7 +228,7 @@ def tile_layered_costmap_spreading_s14_kernel(
             if b == 0 and c0 == 0:
                 sums[k] = ring.tile([P, 2, COLS], F32, name="sums")
             nc.vector.tensor_tensor(
-                out=sums[k][:, b, c0:c1], in0=ps2[k, b][:, c0:c1], in1=base_sb[l][:, c0:c1], op=ADD
+                out=sums[k][:, b, c0:c1], in0=ps2[k, b][:, c0:c1], in1=base_sb[:, l, c0:c1], op=ADD
             )
 
         def finish(k, b0=0, b1=2, c0=0, c1=COLS):
@@ -220,23 +243,32 @@ def tile_layered_costmap_spreading_s14_kernel(
 
         at(-9, setup)
         at(-8, loads)
+        at(-7, turn_vectors)
+        at(-6, spread_base)
         for l in range(LAYERS):
-            for i in range(8):
-                g, t = divmod(i, 4)
-                start, step = (PER_LAYER * l - LEAD, SPAN / 8) if l else (-4, 0.1)
-                at(start + i * step, interleave, l, g, t)
-                if t % 2:
-                    at(start + (i + (2 if l else 1)) * step + 0.001, quantize_grid, l, g, t // 2)
+            for g in range(GROUPS):
+                if l == 0:
+                    for on_scalar, m0, m1 in PIECES_FIRST:
+                        at(-5 + g, interleave, l, g, on_scalar, m0, m1)
+                    for h in (0, 1):
+                        at(-4.9 + g + 0.1 * h, quantize_grid, l, g, 256 * h, 256 * (h + 1))
+                else:
+                    start = PER_LAYER * l - LEAD + g * SPAN / 2
+                    for i, (on_scalar, m0, m1) in enumerate(PIECES):
+                        at(start + i * SPAN / 8, interleave, l, g, on_scalar, m0, m1)
+                    at(start + 3.4 * SPAN / 8, quantize_grid, l, g, 0, COLS)
+        for l in range(LAYERS):
+            at(-3, keep_base, l)
         for k in range(PAIRS):
             last = k == PAIRS - 1
             for b in (0, 1):
                 at(k - 0.95 + 0.01 * b, stage1, k, b)
                 at(k + 0.02 + 0.1 * b, leave, k, b)
                 at(k + 1 + 0.01 * b, stage2, k, b)
-            at(k + 0.6, cap, k)
+            at(k + 0.55, cap, k)
             at(k + 0.8, quantize_capped, k)
             if not last:
-                at(k + 1.4, add_base, k, 0)
+                at(k + 1.7, add_base, k, 0)
                 at(k + 1.9, add_base, k, 1)
                 at(k + 2.3, finish, k)
             else:

from contextlib import ExitStack

import concourse.mybir as mybir
from concourse.masks import make_identity

LAYERS, ROWS, COLS = 4, 1024, 512
FLOPS = 2 * LAYERS * (ROWS * ROWS * COLS + ROWS * COLS * COLS)

F32 = mybir.dt.float32
BF16 = mybir.dt.bfloat16
I32 = mybir.dt.int32
U32 = mybir.dt.uint32
U8 = mybir.dt.uint8
E4M3 = mybir.dt.float8_e4m3fn_x4
E2M1 = mybir.dt.float4_e2m1fn_x4
MIN = mybir.AluOpType.min
ADD = mybir.AluOpType.add
TANH = mybir.ActivationFunctionType.Tanh

P = 128
X4 = 4
GROUPS = ROWS // 512
PAIRS = 16
PER_LAYER = 4

PIECES_FIRST = ((0, 0, 64), (1, 64, 128))
PIECES = ((0, 0, 40), (1, 80, 128), (0, 40, 80))
LEAD, SPAN = 3.9, 2.3
V_DIRECT = ((0, 0), (0, 1), (13, 0), (14, 1))


def tile_layered_costmap_spreading_s14_kernel(
    tc, grid, row_words, row_scales, ceiling, col_words, col_scales, base, out
):
    nc = tc.nc
    steps = []

    def at(key, fn, *args):
        steps.append((key, len(steps), fn, args))

    with ExitStack() as ctx:
        keep = ctx.enter_context(tc.tile_pool(name="keep", bufs=1))
        ring = ctx.enter_context(tc.tile_pool(name="ring", bufs=4))
        psum = ctx.enter_context(tc.psum_pool(name="psum", bufs=4))

        raw = [keep.tile([P, GROUPS, X4, COLS], BF16, name="raw%d" % l, align_bytes=64) for l in range(LAYERS)]
        rw = [keep.tile([P, GROUPS, 2 * ROWS], U8, name="rw%d" % l, align_bytes=64) for l in range(LAYERS)]
        rs0 = keep.tile([P, GROUPS, ROWS], U8, name="rs0", align_bytes=64)
        rs_rest = keep.tile([P, (LAYERS - 1) * GROUPS, ROWS], U8, name="rs_rest", align_bytes=64)
        cw0 = keep.tile([P, 2 * COLS], U8, name="cw0", align_bytes=64)
        cw_rest = keep.tile([P, LAYERS - 1, 2 * COLS], U8, name="cw_rest", align_bytes=64)
        cs = keep.tile([P, LAYERS, COLS], U8, name="cs", align_bytes=64)
        ceil_sb = keep.tile([P, LAYERS, X4], BF16, name="ceil_sb", align_bytes=64)
        base_sb = keep.tile([P, LAYERS, COLS], BF16, name="base_sb", align_bytes=64)
        base_col = keep.tile([P, LAYERS, X4], BF16, name="base_col", align_bytes=64)
        rows = keep.tile([P, COLS], BF16, name="rows", align_bytes=64)
        ident = keep.tile([P, P], BF16, name="ident", align_bytes=64)
        gcodes = [keep.tile([P, GROUPS, COLS], U32, name="gcodes%d" % l, align_bytes=64) for l in range(LAYERS)]
        gscales = [keep.tile([P, GROUPS, COLS], U8, name="gscales%d" % l, align_bytes=64) for l in range(LAYERS)]
        warm = keep.tile([P, 1], F32, name="warm")

        gin = {}
        ps1 = {}
        ps2 = {}
        spread = {}
        capped = {}
        ccodes = {}
        cscales = {}
        sums = {}

        def scale_rows(plane, source, r):
            nc_rows = source.rearrange("g (q r) n -> r q g n", r=4)[r]
            return plane[r:P:32], nc_rows

        def setup():
            nc.vector.memset(rs0[:].rearrange("p g n -> p (g n)").bitcast(U32), 0)
            nc.vector.memset(rows[:].bitcast(U32), 0)
            nc.vector.memset(warm[:], 0.0)
            make_identity(nc, ident[:])
            nc.gpsimd.memset(cs[:].rearrange("p g n -> p (g n)").bitcast(U32), 0)
            nc.gpsimd.memset(rs_rest[:].rearrange("p g n -> p (g n)").bitcast(U32), 0)
            nc.scalar.activation(warm[:], warm[:], TANH)

        def load_scales(engine, plane, source):
            for r in range(4):
                o, i = scale_rows(plane, source, r)
                engine.dma_start(out=o.bitcast(I32), in_=i.bitcast(I32))

        def load_grid(l, g):
            nc.sync.dma_start(
                out=raw[l][:, g], in_=grid[l, 512 * g : 512 * (g + 1), :].rearrange("(p j) c -> p j c", j=X4)
            )

        def load_rows(l):
            nc.sync.dma_start(
                out=rw[l][:], in_=row_words[GROUPS * l : GROUPS * (l + 1)].rearrange("g p n -> p g n")
            )

        def loads():
            nc.sync.dma_start(out=rows[0:LAYERS, :], in_=ceiling)
            nc.sync.dma_start(out=rows[LAYERS : 2 * LAYERS, :], in_=base)
            load_grid(0, 0)
            load_grid(0, 1)
            load_scales(nc.scalar, rs0, row_scales[0:GROUPS])
            load_rows(0)
            load_scales(nc.sync, cs, col_scales)
            nc.sync.dma_start(out=cw0[:], in_=col_words[0])
            load_grid(1, 0)
            load_grid(1, 1)
            load_rows(1)
            load_scales(nc.sync, rs_rest, row_scales[GROUPS:])
            nc.sync.dma_start(out=cw_rest[:], in_=col_words[1:].rearrange("l p n -> p l n"))
            for l in (2, 3):
                load_grid(l, 0)
                load_grid(l, 1)
                load_rows(l)

        def turn_vectors():
            pc = psum.tile([P, X4, P], BF16, name="pc", tag="acc2")
            pb = psum.tile([P, X4, P], BF16, name="pb", tag="acc2")
            for t in range(X4):
                nc.tensor.transpose(pc[:, t, :], rows[:, t:COLS:X4], ident[:])
            for q in range(X4):
                nc.tensor.transpose(pb[:, q, :], rows[:, P * q : P * (q + 1)], ident[:])
            nc.vector.tensor_copy(out=ceil_sb[:], in_=pc[:, :, 0:LAYERS].rearrange("p t l -> p l t"))
            nc.vector.tensor_copy(out=base_col[:], in_=pb[:, :, LAYERS : 2 * LAYERS].rearrange("p q l -> p l q"))

        spreadb = {}

        def spread_base():
            for l in range(LAYERS):
                ps = psum.tile([P, X4, P], BF16, name="ps", tag="acc2")
                spreadb[l] = ps
                for q in range(X4):
                    nc.tensor.transpose(ps[:, q, :], base_col[:, l, q : q + 1].to_broadcast([P, P]), ident[:])

        def keep_base(l):
            copy = nc.scalar.copy if l % 2 else nc.vector.tensor_copy
            copy(out=base_sb[:, l, :], in_=spreadb[l][:].rearrange("p q n -> p (q n)"))

        def interleave(l, g, on_scalar, m0, m1):
            if (l, g) not in gin:
                gin[l, g] = ring.tile([P, X4, P, X4], BF16, name="gin", align_bytes=64)
            dst = gin[l, g][:, :, m0:m1, :].rearrange("p t m j -> p m j t")
            src = raw[l][:, g].rearrange("p j (m t) -> p m j t", t=X4)[:, m0:m1]
            if on_scalar:
                nc.scalar.copy(out=dst, in_=src)
            else:
                nc.vector.tensor_copy(out=dst, in_=src)

        def quantize_grid(l, g, c0, c1):
            nc.vector.quantize_mx(
                out=gcodes[l][:, g, c0:c1].bitcast(E4M3),
                scales=gscales[l][:, g, c0:c1],
                in_=gin[l, g][:].rearrange("p t m j -> p (t m j)")[:, X4 * c0 : X4 * c1],
            )

        def stage1(k, b):
            l = k // PER_LAYER
            n0 = 256 * (k % PER_LAYER) + P * b
            acc = psum.tile([P, X4, P], F32, name="acc1")
            ps1[k, b] = acc
            for t in range(X4):
                for g in range(GROUPS):
                    plane = rs0[:, g, n0 : n0 + P] if l == 0 else rs_rest[:, GROUPS * (l - 1) + g, n0 : n0 + P]
                    nc.tensor.matmul_mx(
                        out=acc[:, t, :],
                        lhsT=gcodes[l][:, g, P * t : P * (t + 1)].bitcast(E4M3),
                        lhsT_scale=gscales[l][:, g, P * t : P * (t + 1)],
                        rhs=rw[l][:, g, 2 * n0 : 2 * (n0 + P)].bitcast(E2M1),
                        rhs_scale=plane,
                        start=(g == 0),
                        stop=(g == GROUPS - 1),
                    )

        def leave(k, b):
            l = k // PER_LAYER
            if b == 0:
                capped[k] = ring.tile([P, 2, P, X4], BF16, name="capped", align_bytes=64)
                spread[k] = ring.tile([P, 2, P, X4], BF16, name="spread", align_bytes=64)
            src = ps1[k, b][:].rearrange("p t n -> p n t")
            if (k, b) in V_DIRECT:
                nc.vector.tensor_tensor(
                    out=capped[k][:, b], in0=src, in1=ceil_sb[:, l, :].unsqueeze(1).to_broadcast([P, P, X4]), op=MIN
                )
            else:
                nc.scalar.copy(out=spread[k][:, b], in_=src)

        def cap(k):
            l = k // PER_LAYER
            bs = [b for b in (0, 1) if (k, b) not in V_DIRECT]
            if bs:
                lo, hi = bs[0], bs[-1] + 1
                n = P * (hi - lo)
                nc.vector.tensor_tensor(
                    out=capped[k][:, lo:hi].rearrange("p b n t -> p (b n) t"),
                    in0=spread[k][:, lo:hi].rearrange("p b n t -> p (b n) t"),
                    in1=ceil_sb[:, l, :].unsqueeze(1).to_broadcast([P, n, X4]),
                    op=MIN,
                )

        def quantize_capped(k):
            ccodes[k] = ring.tile([P, 2 * P], U32, name="ccodes", align_bytes=64)
            cscales[k] = ring.tile([P, 2 * P], U8, name="cscales", align_bytes=64)
            nc.vector.quantize_mx(
                out=ccodes[k][:].bitcast(E4M3),
                scales=cscales[k][:],
                in_=capped[k][:].rearrange("p b n t -> p (b n t)"),
            )

        def stage2(k, b):
            l = k // PER_LAYER
            acc = psum.tile([P, COLS], F32, name="acc2")
            ps2[k, b] = acc
            words = cw0[:] if l == 0 else cw_rest[:, l - 1, :]
            nc.tensor.matmul_mx(
                out=acc[:],
                lhsT=ccodes[k][:, P * b : P * (b + 1)].bitcast(E4M3),
                lhsT_scale=cscales[k][:, P * b : P * (b + 1)],
                rhs=words.bitcast(E2M1),
                rhs_scale=cs[:, l, :],
                start=True,
                stop=True,
            )

        def add_base(k, b, c0=0, c1=COLS):
            l = k // PER_LAYER
            if b == 0 and c0 == 0:
                sums[k] = ring.tile([P, 2, COLS], F32, name="sums")
            nc.vector.tensor_tensor(
                out=sums[k][:, b, c0:c1], in0=ps2[k, b][:, c0:c1], in1=base_sb[:, l, c0:c1], op=ADD
            )

        def finish(k, b0=0, b1=2, c0=0, c1=COLS):
            l = k // PER_LAYER
            r0 = 256 * (k % PER_LAYER)
            res = ring.tile([P, 2, COLS], F32, name="res")
            nc.scalar.activation(res[:, b0:b1, c0:c1], sums[k][:, b0:b1, c0:c1], TANH)
            nc.sync.dma_start(
                out=out[l, r0 + P * b0 : r0 + P * b1, c0:c1].rearrange("(b p) c -> p b c", p=P),
                in_=res[:, b0:b1, c0:c1],
            )

        at(-9, setup)
        at(-8, loads)
        at(-7, turn_vectors)
        at(-6, spread_base)
        for l in range(LAYERS):
            for g in range(GROUPS):
                if l == 0:
                    for on_scalar, m0, m1 in PIECES_FIRST:
                        at(-5 + g, interleave, l, g, on_scalar, m0, m1)
                    for h in (0, 1):
                        at(-4.9 + g + 0.1 * h, quantize_grid, l, g, 256 * h, 256 * (h + 1))
                else:
                    start = PER_LAYER * l - LEAD + g * SPAN / 2
                    for i, (on_scalar, m0, m1) in enumerate(PIECES):
                        at(start + i * SPAN / 8, interleave, l, g, on_scalar, m0, m1)
                    at(start + 3.4 * SPAN / 8, quantize_grid, l, g, 0, COLS)
        for l in range(LAYERS):
            at(-3, keep_base, l)
        for k in range(PAIRS):
            last = k == PAIRS - 1
            for b in (0, 1):
                at(k - 0.95 + 0.01 * b, stage1, k, b)
                at(k + 0.02 + 0.1 * b, leave, k, b)
                at(k + 1 + 0.01 * b, stage2, k, b)
            at(k + 0.55, cap, k)
            at(k + 0.8, quantize_capped, k)
            if not last:
                at(k + 1.7, add_base, k, 0)
                at(k + 1.9, add_base, k, 1)
                at(k + 2.3, finish, k)
            else:
                for i, (b, c0, c1) in enumerate(((0, 0, 512), (1, 0, 256), (1, 256, 512))):
                    at(k + 2.4 + 0.1 * i, add_base, k, b, c0, c1)
                    at(k + 2.45 + 0.1 * i, finish, k, b, b + 1, c0, c1)

        with tc.manual_schedule():
            for key, order, fn, args in sorted(steps, key=lambda s: s[:2]):
                fn(*args)
